import numpy as np
import ml_dtypes

BF16 = ml_dtypes.bfloat16


def bf(x):
    return np.asarray(x, np.float32).astype(BF16)


def f32(x):
    return np.asarray(x, np.float32)


def f64(x):
    return np.asarray(x).astype(np.float64)


def striped(idx):
    return np.tile(idx.reshape(-1, 16).T, (8, 1))


def rows(idx, k):
    return np.tile(idx, (k, 1))


def look(tab, idx):
    return np.take_along_axis(f64(tab), rows(idx, len(tab)), axis=1)


K, S, V, N, M = 512, 2048, 1024, 1024, 128


def setup_inputs():
    return {"tab": f32(np.random.standard_normal((2, K, S))), "y": f32(np.random.standard_normal((K, V))), "w": bf(np.random.standard_normal((K, M)) / np.sqrt(K)), "b": f32(0.5 * np.random.standard_normal((M, 1))), "offs": striped(np.random.permutation(S)[:N])}


def reference(tab, y, w, b, offs):
    idx = offs[:16].T.reshape(-1)
    x = (look(tab[0], idx) + f64(y)) * (np.tanh(look(tab[1], idx)))
    return np.maximum(f64(w).T @ x + f64(b), 0.0)

@@ -1,0 +1,58 @@
+import concourse.mybir as mybir
+
+BF16, F32, U16 = mybir.dt.bfloat16, mybir.dt.float32, mybir.dt.uint16
+ADD, MULT, MAX = mybir.AluOpType.add, mybir.AluOpType.mult, mybir.AluOpType.max
+TANH = mybir.ActivationFunctionType.Tanh
+
+P = 128
+ROWS, PLACES, PICKS, OUT_ROWS = 512, 2048, 1024, 128
+BLOCKS = ROWS // P
+PIECE = 512
+PER_COLUMN = 16
+
+FLOPS = 2 * ROWS * PICKS * OUT_ROWS
+
+
+def tile_lookup_vg_addtanh_relu_kernel(tc, tab, y, w, b, offs, out):
+    nc = tc.nc
+    tab_blocks = tab.rearrange("t (p k) s -> t k p s", k=BLOCKS)
+    y_blocks = y.rearrange("(p k) n -> k p n", k=BLOCKS)
+    w_rows = w.rearrange("(p k) m -> p (k m)", k=BLOCKS)
+    with (
+        tc.tile_pool(name="held", bufs=1) as held,
+        tc.tile_pool(name="loads", bufs=BLOCKS) as loads,
+        tc.tile_pool(name="work", bufs=3) as work,
+        tc.psum_pool(name="psum", bufs=1) as psum,
+    ):
+        offsets = held.tile([P, PICKS // PER_COLUMN], U16, name="offsets")
+        nc.sync.dma_start(offsets[:], offs)
+        weights = held.tile([P, BLOCKS * OUT_ROWS], BF16, name="weights")
+        nc.scalar.dma_start(weights[:], w_rows)
+        bias = held.tile([P, 1], F32, name="bias")
+        nc.scalar.dma_start(bias[:], b)
+
+        pieces = [slice(a, a + PIECE) for a in range(0, PICKS, PIECE)]
+        sums = [psum.tile([P, PIECE], F32, name=f"sums{i}") for i in range(len(pieces))]
+
+        for k in range(BLOCKS):
+            stream = loads.tile([P, PICKS], F32, name="stream")
+            nc.sync.dma_start(stream[:], y_blocks[k])
+            values = loads.tile([P, PLACES], F32, name="values")
+            nc.sync.dma_start(values[:], tab_blocks[0, k])
+            gates = loads.tile([P, PLACES], F32, name="gates")
+            nc.sync.dma_start(gates[:], tab_blocks[1, k])
+            for i, piece in enumerate(pieces):
+                listed = offsets[:, piece.start // PER_COLUMN : piece.stop // PER_COLUMN]
+                shifted = work.tile([P, PIECE], F32, name="shifted")
+                nc.vector.tensor_tensor(shifted[:], values[:].indirect(listed), stream[:, piece], ADD)
+                opened = work.tile([P, PIECE], F32, name="opened")
+                nc.scalar.activation(opened[:], gates[:].indirect(listed), TANH)
+                x = work.tile([P, PIECE], BF16, name="x")
+                nc.vector.tensor_tensor(x[:], shifted[:], opened[:], MULT)
+                w_block = weights[:, k * OUT_ROWS : (k + 1) * OUT_ROWS]
+                nc.tensor.matmul(sums[i][:], w_block, x[:], start=k == 0, stop=k == BLOCKS - 1)
+
+        for i, piece in enumerate(pieces):
+            result = work.tile([P, PIECE], F32, name="result")
+            nc.vector.tensor_scalar(result[:], sums[i][:], bias[:], 0.0, ADD, MAX)
+            nc.sync.dma_start(out[:, piece], result[:])

@@ -7,7 +7,7 @@ TANH = mybir.ActivationFunctionType.Tanh
 P = 128
 ROWS, PLACES, PICKS, OUT_ROWS = 512, 2048, 1024, 128
 BLOCKS = ROWS // P
-PIECE = 512
+PIECE = 256
 PER_COLUMN = 16
 
 FLOPS = 2 * ROWS * PICKS * OUT_ROWS
@@ -16,12 +16,13 @@ FLOPS = 2 * ROWS * PICKS * OUT_ROWS
 def tile_lookup_vg_addtanh_relu_kernel(tc, tab, y, w, b, offs, out):
     nc = tc.nc
     tab_blocks = tab.rearrange("t (p k) s -> t k p s", k=BLOCKS)
-    y_blocks = y.rearrange("(p k) n -> k p n", k=BLOCKS)
+    y_rows = y.rearrange("(p k) n -> p (k n)", k=BLOCKS)
     w_rows = w.rearrange("(p k) m -> p (k m)", k=BLOCKS)
     with (
         tc.tile_pool(name="held", bufs=1) as held,
         tc.tile_pool(name="loads", bufs=BLOCKS) as loads,
-        tc.tile_pool(name="work", bufs=3) as work,
+        tc.tile_pool(name="work", bufs=2) as work,
+        tc.tile_pool(name="results", bufs=PICKS // PIECE) as results,
         tc.psum_pool(name="psum", bufs=1) as psum,
     ):
         offsets = held.tile([P, PICKS // PER_COLUMN], U16, name="offsets")
@@ -34,25 +35,28 @@ def tile_lookup_vg_addtanh_relu_kernel(tc, tab, y, w, b, offs, out):
         pieces = [slice(a, a + PIECE) for a in range(0, PICKS, PIECE)]
         sums = [psum.tile([P, PIECE], F32, name=f"sums{i}") for i in range(len(pieces))]
 
+        stream = held.tile([P, BLOCKS * PICKS], F32, name="stream")
         for k in range(BLOCKS):
-            stream = loads.tile([P, PICKS], F32, name="stream")
-            nc.sync.dma_start(stream[:], y_blocks[k])
             values = loads.tile([P, PLACES], F32, name="values")
             nc.sync.dma_start(values[:], tab_blocks[0, k])
             gates = loads.tile([P, PLACES], F32, name="gates")
             nc.sync.dma_start(gates[:], tab_blocks[1, k])
+            if k == 0:
+                nc.sync.dma_start(stream[:], y_rows)
+            shifted = work.tile([P, PICKS], F32, name="shifted")
+            opened = work.tile([P, PICKS], F32, name="opened")
+            x = work.tile([P, PICKS], BF16, name="x")
+            y_block = stream[:, k * PICKS : (k + 1) * PICKS]
+            w_block = weights[:, k * OUT_ROWS : (k + 1) * OUT_ROWS]
+            for span in pieces if k == BLOCKS - 1 else [slice(0, PICKS)]:
+                listed = offsets[:, span.start // PER_COLUMN : span.stop // PER_COLUMN]
+                nc.vector.tensor_tensor(shifted[:, span], values[:].indirect(listed), y_block[:, span], ADD)
+                nc.scalar.activation(opened[:, span], gates[:].indirect(listed), TANH)
+                nc.vector.tensor_tensor(x[:, span], shifted[:, span], opened[:, span], MULT)
             for i, piece in enumerate(pieces):
-                listed = offsets[:, piece.start // PER_COLUMN : piece.stop // PER_COLUMN]
-                shifted = work.tile([P, PIECE], F32, name="shifted")
-                nc.vector.tensor_tensor(shifted[:], values[:].indirect(listed), stream[:, piece], ADD)
-                opened = work.tile([P, PIECE], F32, name="opened")
-                nc.scalar.activation(opened[:], gates[:].indirect(listed), TANH)
-                x = work.tile([P, PIECE], BF16, name="x")
-                nc.vector.tensor_tensor(x[:], shifted[:], opened[:], MULT)
-                w_block = weights[:, k * OUT_ROWS : (k + 1) * OUT_ROWS]
-                nc.tensor.matmul(sums[i][:], w_block, x[:], start=k == 0, stop=k == BLOCKS - 1)
+                nc.tensor.matmul(sums[i][:], w_block, x[:, piece], start=k == 0, stop=k == BLOCKS - 1)
 
         for i, piece in enumerate(pieces):
-            result = work.tile([P, PIECE], F32, name="result")
+            result = results.tile([P, PIECE], F32, name="result")
             nc.vector.tensor_scalar(result[:], sums[i][:], bias[:], 0.0, ADD, MAX)
             nc.sync.dma_start(out[:, piece], result[:])

@@ -39,10 +39,10 @@ def tile_lookup_vg_addtanh_relu_kernel(tc, tab, y, w, b, offs, out):
         for k in range(BLOCKS):
             values = loads.tile([P, PLACES], F32, name="values")
             nc.sync.dma_start(values[:], tab_blocks[0, k])
-            gates = loads.tile([P, PLACES], F32, name="gates")
-            nc.sync.dma_start(gates[:], tab_blocks[1, k])
             if k == 0:
                 nc.sync.dma_start(stream[:], y_rows)
+            gates = loads.tile([P, PLACES], F32, name="gates")
+            nc.sync.dma_start(gates[:], tab_blocks[1, k])
             shifted = work.tile([P, PICKS], F32, name="shifted")
             opened = work.tile([P, PICKS], F32, name="opened")
             x = work.tile([P, PICKS], BF16, name="x")

import concourse.mybir as mybir

BF16, F32, U16 = mybir.dt.bfloat16, mybir.dt.float32, mybir.dt.uint16
ADD, MULT, MAX = mybir.AluOpType.add, mybir.AluOpType.mult, mybir.AluOpType.max
TANH = mybir.ActivationFunctionType.Tanh

P = 128
ROWS, PLACES, PICKS, OUT_ROWS = 512, 2048, 1024, 128
BLOCKS = ROWS // P
PIECE = 256
PER_COLUMN = 16

FLOPS = 2 * ROWS * PICKS * OUT_ROWS


def tile_lookup_vg_addtanh_relu_kernel(tc, tab, y, w, b, offs, out):
    nc = tc.nc
    tab_blocks = tab.rearrange("t (p k) s -> t k p s", k=BLOCKS)
    y_rows = y.rearrange("(p k) n -> p (k n)", k=BLOCKS)
    w_rows = w.rearrange("(p k) m -> p (k m)", k=BLOCKS)
    with (
        tc.tile_pool(name="held", bufs=1) as held,
        tc.tile_pool(name="loads", bufs=BLOCKS) as loads,
        tc.tile_pool(name="work", bufs=2) as work,
        tc.tile_pool(name="results", bufs=PICKS // PIECE) as results,
        tc.psum_pool(name="psum", bufs=1) as psum,
    ):
        offsets = held.tile([P, PICKS // PER_COLUMN], U16, name="offsets")
        nc.sync.dma_start(offsets[:], offs)
        weights = held.tile([P, BLOCKS * OUT_ROWS], BF16, name="weights")
        nc.scalar.dma_start(weights[:], w_rows)
        bias = held.tile([P, 1], F32, name="bias")
        nc.scalar.dma_start(bias[:], b)

        pieces = [slice(a, a + PIECE) for a in range(0, PICKS, PIECE)]
        sums = [psum.tile([P, PIECE], F32, name=f"sums{i}") for i in range(len(pieces))]

        stream = held.tile([P, BLOCKS * PICKS], F32, name="stream")
        for k in range(BLOCKS):
            values = loads.tile([P, PLACES], F32, name="values")
            nc.sync.dma_start(values[:], tab_blocks[0, k])
            if k == 0:
                nc.sync.dma_start(stream[:], y_rows)
            gates = loads.tile([P, PLACES], F32, name="gates")
            nc.sync.dma_start(gates[:], tab_blocks[1, k])
            shifted = work.tile([P, PICKS], F32, name="shifted")
            opened = work.tile([P, PICKS], F32, name="opened")
            x = work.tile([P, PICKS], BF16, name="x")
            y_block = stream[:, k * PICKS : (k + 1) * PICKS]
            w_block = weights[:, k * OUT_ROWS : (k + 1) * OUT_ROWS]
            for span in pieces if k == BLOCKS - 1 else [slice(0, PICKS)]:
                listed = offsets[:, span.start // PER_COLUMN : span.stop // PER_COLUMN]
                nc.vector.tensor_tensor(shifted[:, span], values[:].indirect(listed), y_block[:, span], ADD)
                nc.scalar.activation(opened[:, span], gates[:].indirect(listed), TANH)
                nc.vector.tensor_tensor(x[:, span], shifted[:, span], opened[:, span], MULT)
            for i, piece in enumerate(pieces):
                nc.tensor.matmul(sums[i][:], w_block, x[:, piece], start=k == 0, stop=k == BLOCKS - 1)

        for i, piece in enumerate(pieces):
            result = results.tile([P, PIECE], F32, name="result")
            nc.vector.tensor_scalar(result[:], sums[i][:], bias[:], 0.0, ADD, MAX)
            nc.sync.dma_start(out[:, piece], result[:])
